import numpy as np
import ml_dtypes


def mxq(x, axis, fmt="e4m3"):
    dtype, down = {"e4m3": (ml_dtypes.float8_e4m3fn, 7), "e5m2": (ml_dtypes.float8_e5m2, 14)}[fmt]
    v = np.moveaxis(np.asarray(x, np.float32).astype(ml_dtypes.bfloat16).astype(np.float64), axis, -1)
    blocks = v.reshape(v.shape[:-1] + (-1, 32))
    amax = np.abs(blocks).max(-1, keepdims=True)
    byte = np.maximum(np.where(amax > 0, np.frexp(amax)[1] - 1 + 127, 0) - down, 1)
    scale = np.exp2(byte - 127.0)
    codes = (blocks / scale).astype(np.float32).astype(dtype).astype(np.float64)
    return np.moveaxis((codes * scale).reshape(v.shape), -1, axis)


WIDE = False


def mx_kscale(k):
    if not WIDE:
        return np.ones(k)
    levels = np.array([30, -30])
    if k % 512:
        return np.exp2(np.random.permutation(np.resize(levels, k // 32))).repeat(32)
    a = np.empty((k // 512, 16))
    for p in range(k // 512):
        a[p, :8] = np.random.permutation(np.resize(levels, 8))
        for g in range(8):
            far = levels[np.abs(levels - a[p, g]) >= 10]
            a[p, g + 8] = far[np.random.randint(len(far))]
    return np.exp2(a.ravel()).repeat(32)


BF16 = ml_dtypes.bfloat16


def bf(x):
    return np.asarray(x, np.float32).astype(BF16)


def f64(x):
    return np.asarray(x).astype(np.float64)


N, R, L, M = 1024, 1024, 1024, 2048


def setup_inputs():
    s = mx_kscale(L)
    t = mx_kscale(M)
    b = 0.5 * np.random.standard_normal(M)
    slack = 0.1 + np.square(np.random.standard_normal((M, R)))
    return {"e": bf(np.random.standard_normal((R, L)) * s),
            "f": bf(np.random.standard_normal((L, N)) / np.sqrt(L) / s[:, None]),
            "ax": bf((b[:, None] - slack) / t[:, None]),
            "b": bf(b / t),
            "mu": bf(0.2 + 0.2 * np.random.random(R)),
            "a": bf(np.random.standard_normal((M, N)) / np.sqrt(M) / t[:, None]),
            "c": bf(0.3 * np.random.standard_normal(N))}


def reference(e, f, ax, b, mu, a, c):
    slack = f64(b)[:, None] - f64(ax)
    lam = f64(mu)[None, :] / slack
    fq = mxq(f64(f), 0, "e4m3")
    eq = mxq(f64(e), 1, "e4m3")
    aq = mxq(f64(a), 0, "e4m3")
    lq = mxq(lam, 0, "e5m2")
    g = (fq.T @ eq.T) + (aq.T @ lq)
    return g + f64(c)[:, None]

@@ -1,0 +1,318 @@
+from contextlib import ExitStack
+
+import concourse.mybir as mybir
+from concourse.masks import make_identity
+
+N, R, L, M = 1024, 1024, 1024, 2048
+FLOPS = 2 * N * R * (L + M)
+BYTES = 2 * (R * L + L * N + M * R + M + R + M * N + N) + 4 * N * R
+
+F32 = mybir.dt.float32
+BF16 = mybir.dt.bfloat16
+U32 = mybir.dt.uint32
+U8 = mybir.dt.uint8
+E4M3 = mybir.dt.float8_e4m3fn_x4
+E5M2 = mybir.dt.float8_e5m2_x4
+ALU = mybir.AluOpType
+ACT = mybir.ActivationFunctionType
+
+P = 128
+PACK = 4
+H = 512
+NT = N // P
+
+
+def tile_log_barrier_gradient_s2_kernel(tc, e, f, ax, b, mu, a, c, out):
+    nc = tc.nc
+    with ExitStack() as ctx:
+        const = ctx.enter_context(tc.tile_pool(name="const", bufs=1))
+        raw = ctx.enter_context(tc.tile_pool(name="raw", bufs=1))
+        keep = ctx.enter_context(tc.tile_pool(name="keep", bufs=1))
+        stage = ctx.enter_context(tc.tile_pool(name="stage", bufs=3))
+        psum = ctx.enter_context(tc.psum_pool(name="psum", bufs=1))
+        ctx.enter_context(tc.manual_schedule())
+
+        rows = const.tile([P, P], BF16, name="rows")
+        nc.vector.memset(rows[:], 0.0)
+        bcol = const.tile([P, 4, PACK], BF16, name="bcol")
+        warm = const.tile([P, 1], F32, name="warm")
+        nc.scalar.dma_start(out=rows[0:8, :], in_=mu.rearrange("(t m) -> t m", m=P))
+        nc.scalar.dma_start(out=rows[8:16, :], in_=c.rearrange("(t m) -> t m", m=P))
+        nc.scalar.dma_start(out=bcol[:], in_=b.rearrange("(g p j) -> p g j", p=P, j=PACK))
+        ident_b = const.tile([P, P], BF16, name="ident_b")
+        make_identity(nc, ident_b[:])
+        ident_f = const.tile([P, P], F32, name="ident_f")
+        make_identity(nc, ident_f[:])
+        nc.vector.memset(warm[:], 1.0)
+        nc.scalar.activation(out=warm[:], in_=warm[:], func=ACT.Abs_reciprocal_sqrt)
+
+        fraw = {}
+        araw = {}
+        eraw = {}
+        axraw = {}
+
+        def load_f(g, hh):
+            t = raw.tile([P, PACK, H], BF16, name=f"f{g}{hh}")
+            nc.sync.dma_start(
+                out=t[:],
+                in_=f[512 * g : 512 * (g + 1), H * hh : H * (hh + 1)].rearrange("(p j) n -> p j n", j=PACK),
+            )
+            fraw[(g, hh)] = t
+
+        def load_a(g):
+            t = raw.tile([P, PACK, N], BF16, name=f"a{g}", tag="raw8", bufs=4)
+            nc.sync.dma_start(out=t[:], in_=a[512 * g : 512 * (g + 1), :].rearrange("(p j) n -> p j n", j=PACK))
+            araw[g] = t
+
+        def load_e(h):
+            t = raw.tile([P, 4, L], BF16, name=f"e{h}", tag="raw8", bufs=4)
+            nc.sync.dma_start(out=t[:], in_=e[512 * h : 512 * (h + 1), :].rearrange("(t p) l -> p t l", p=P))
+            eraw[h] = t
+
+        def load_ax(k):
+            g, h = k % 4, k // 4
+            t = raw.tile([P, PACK, H], BF16, name=f"ax{k}", tag="ax", bufs=6)
+            nc.sync.dma_start(
+                out=t[:],
+                in_=ax[512 * g : 512 * (g + 1), H * h : H * (h + 1)].rearrange("(p j) r -> p j r", j=PACK),
+            )
+            axraw[k] = t
+
+        load_f(0, 0)
+        load_ax(0)
+        load_f(0, 1)
+        load_e(0)
+        load_ax(1)
+        load_f(1, 0)
+        load_f(1, 1)
+        load_e(1)
+        load_a(0)
+        load_ax(2)
+        load_a(1)
+        load_ax(3)
+        load_a(2)
+        load_ax(4)
+        load_a(3)
+        load_ax(5)
+
+        fc = [keep.tile([P, N], U32, name=f"fc{g}", align_bytes=64) for g in range(2)]
+        fs = [keep.tile([P, N], U8, name=f"fs{g}", align_bytes=64) for g in range(2)]
+        ac = [keep.tile([P, N], U32, name=f"ac{g}", align_bytes=64) for g in range(4)]
+        asc = [keep.tile([P, N], U8, name=f"as{g}", align_bytes=64) for g in range(4)]
+        ec = [keep.tile([P, R], U32, name=f"ec{g}", align_bytes=64) for g in range(2)]
+        es = [keep.tile([P, R], U8, name=f"es{g}", align_bytes=64) for g in range(2)]
+        lc = [keep.tile([P, R], U32, name=f"lc{g}", align_bytes=64) for g in range(4)]
+        ls = [keep.tile([P, R], U8, name=f"ls{g}", align_bytes=64) for g in range(4)]
+        qrow = const.tile([P, R], F32, name="qrow")
+        qcol = const.tile([P, 8], F32, name="qcol")
+        ccol = const.tile([P, 8], F32, name="ccol")
+
+        def bank(i, shape, dtype, nm):
+            return psum.tile(shape, dtype, name=nm, tag=f"bank{i}")
+
+        vt = bank(0, [P, P], BF16, "vt")
+        nc.tensor.transpose(vt[:], rows[:], ident_b[:])
+        nc.vector.reciprocal(out=qcol[:], in_=vt[:, 0:8])
+        nc.vector.tensor_copy(out=ccol[:], in_=vt[:, 8:16])
+        for hh in range(2):
+            qp = bank(1 + hh, [P, H], F32, f"qp{hh}")
+            for t in range(4):
+                nc.tensor.transpose(
+                    qp[:, P * t : P * (t + 1)],
+                    qcol[:, 4 * hh + t : 4 * hh + t + 1].to_broadcast([P, P]),
+                    ident_f[:],
+                )
+            nc.scalar.copy(out=qrow[:, H * hh : H * (hh + 1)], in_=qp[:])
+
+        grouped = {}
+        egr = {}
+        xts = {}
+        wt = {}
+        yt = {}
+        rt = {}
+        tt = {}
+        lam = {}
+        acc = {}
+
+        def unit(u):
+            if u < 4:
+                return fraw[(u // 2, u % 2)][:], fc[u // 2], fs[u // 2], u % 2
+            v = u - 4
+            return araw[v // 2][:, :, H * (v % 2) : H * (v % 2 + 1)], ac[v // 2], asc[v // 2], v % 2
+
+        def step_I(eng, u):
+            src = unit(u)[0]
+            g = stage.tile([P, H, PACK], BF16, name=f"grp{u}", tag="grp" + eng, bufs=2 if eng == "V" else 3, align_bytes=64)
+            grouped[u] = g
+            o = g[:].rearrange("p (w i) t -> p w t i", i=4)
+            i = src.rearrange("p t (w i) -> p w t i", i=4)
+            if eng == "V":
+                nc.vector.tensor_copy(out=o, in_=i)
+            else:
+                nc.scalar.copy(out=o, in_=i)
+
+        def quantize(codes, scales, hh, fmt, src):
+            cols = slice(H * hh, H * (hh + 1))
+            nc.vector.quantize_mx(
+                out=codes[:, cols].bitcast(fmt), scales=scales[:, cols], in_=src[:].rearrange("p w t -> p (w t)")
+            )
+
+        def step_Q(eng, u):
+            _, codes, scales, hh = unit(u)
+            quantize(codes, scales, hh, E4M3, grouped.pop(u))
+
+        def step_tr(eng, h, g, pr):
+            words = eraw[h][:].rearrange("p t l -> p (t l)").bitcast(F32).rearrange("p (t w) -> p t w", t=4)
+            x = bank(4 * h + 2 * g + pr, [P, 2, 256], F32, f"xt{h}{g}{pr}")
+            xts[(h, g, pr)] = x
+            for t in range(2):
+                for u in range(2):
+                    nc.tensor.transpose(
+                        x[:, u, P * t : P * (t + 1)],
+                        words[:, 2 * pr + t, 256 * g + u : 256 * (g + 1) : 2],
+                        ident_f[:],
+                    )
+
+        def step_d(eng, h, g, pr):
+            if pr == 0:
+                egr[(h, g)] = stage.tile([P, H, PACK], BF16, name=f"eg{h}{g}", tag="eg", bufs=2, align_bytes=64)
+            nc.scalar.copy(
+                out=egr[(h, g)][:, 256 * pr : 256 * (pr + 1), :]
+                .rearrange("p r t -> p (r t)")
+                .bitcast(F32)
+                .rearrange("p (r u) -> p r u", u=2),
+                in_=xts.pop((h, g, pr))[:].rearrange("p u r -> p r u"),
+            )
+
+        def step_eq(eng, h, g):
+            quantize(ec[g], es[g], h, E4M3, egr.pop((h, g)))
+
+        def step_w(eng, k):
+            g, h = k % 4, k // 4
+            w = stage.tile([P, PACK, H], F32, name=f"w{k}", tag="w", bufs=3)
+            wt[k] = w
+            for j in range(PACK):
+                nc.vector.scalar_tensor_tensor(
+                    out=w[:, j, :],
+                    in0=axraw[k][:, j, :],
+                    scalar=bcol[:, g, j : j + 1],
+                    in1=qrow[:, H * h : H * (h + 1)],
+                    op0=ALU.subtract,
+                    op1=ALU.mult,
+                )
+
+        def step_Y(eng, k):
+            y = stage.tile([P, PACK, H], F32, name=f"y{k}", tag="y", bufs=1)
+            yt[k] = y
+            nc.scalar.activation(out=y[:], in_=wt[k][:], func=ACT.Abs_reciprocal_sqrt, scale=-1.0)
+
+        def step_r(eng, k):
+            r = stage.tile([P, H, PACK], F32, name=f"r{k}", tag="r", bufs=2)
+            rt[k] = r
+            nc.scalar.activation(
+                out=r[:].rearrange("p (w i) t -> p w t i", i=4),
+                in_=yt.pop(k)[:].rearrange("p t (w i) -> p w t i", i=4),
+                func=ACT.Square,
+            )
+
+        def step_t(eng, k):
+            t = stage.tile([P, H, PACK], F32, name=f"t{k}", tag="t", bufs=1)
+            tt[k] = t
+            nc.vector.tensor_tensor(
+                out=t[:], in0=wt.pop(k)[:].rearrange("p t w -> p w t"), in1=rt[k][:], op=ALU.mult
+            )
+
+        def step_l(eng, k):
+            lt = stage.tile([P, H, PACK], BF16, name=f"lam{k}", tag="lam", bufs=2, align_bytes=64)
+            lam[k] = lt
+            nc.vector.scalar_tensor_tensor(
+                out=lt[:], in0=tt.pop(k)[:], scalar=2.0, in1=rt.pop(k)[:], op0=ALU.add, op1=ALU.mult
+            )
+
+        def step_lq(eng, k):
+            quantize(lc[k % 4], ls[k % 4], k // 4, E5M2, lam.pop(k))
+
+        def step_mm(eng, t, h, kind, g):
+            if kind == "f":
+                if g == 0:
+                    acc[(t, h)] = bank(t, [P, H], F32, f"acc{t}{h}")
+                st, ss, mv, ms, dt = fc[g], fs[g], ec[g], es[g], E4M3
+            else:
+                st, ss, mv, ms, dt = ac[g], asc[g], lc[g], ls[g], E5M2
+            mc = slice(P * t, P * (t + 1))
+            rc = slice(H * h, H * (h + 1))
+            nc.tensor.matmul_mx(
+                out=acc[(t, h)][:],
+                lhsT=st[:, mc].bitcast(E4M3),
+                lhsT_scale=ss[:, mc],
+                rhs=mv[:, rc].bitcast(dt),
+                rhs_scale=ms[:, rc],
+                start=(kind == "f" and g == 0),
+                stop=(kind == "a" and g == 3),
+            )
+
+        def step_ev(eng, t, h):
+            o = stage.tile([P, H], F32, name=f"o{t}{h}", tag="o", bufs=4)
+            if eng == "V":
+                nc.vector.tensor_scalar(
+                    out=o[:], in0=acc[(t, h)][:], scalar1=ccol[:, t : t + 1], scalar2=None, op0=ALU.add
+                )
+            else:
+                nc.scalar.activation(
+                    out=o[:], in_=acc[(t, h)][:], func=ACT.Identity, bias=ccol[:, t : t + 1]
+                )
+            nc.sync.dma_start(out=out[P * t : P * (t + 1), H * h : H * (h + 1)], in_=o[:])
+
+        steps = {
+            "I": step_I, "Q": step_Q, "tr": step_tr, "d": step_d, "eq": step_eq, "w": step_w, "Y": step_Y,
+            "r": step_r, "t": step_t, "l": step_l, "lq": step_lq, "mm": step_mm, "ev": step_ev,
+        }
+
+        queues = {
+            "V": [("I", 0), ("Q", 0), ("w", 0), ("Q", 1), ("w", 1), ("I", 3), ("t", 0), ("Q", 3), ("l", 0), ("eq", 0, 0), ("eq", 0, 1), ("lq", 0), ("Q", 2), ("w", 2), ("w", 3), ("t", 1), ("eq", 1, 0), ("eq", 1, 1), ("l", 1), ("I", 6), ("lq", 1), ("Q", 4), ("t", 2), ("Q", 5), ("l", 2), ("w", 4), ("lq", 2), ("Q", 6), ("Q", 7), ("t", 3), ("w", 5), ("l", 3), ("Q", 8), ("lq", 3), ("Q", 9), ("t", 4), ("Q", 10), ("w", 6), ("l", 4), ("Q", 11), ("lq", 4), ("t", 5), ("w", 7), ("l", 5), ("t", 6), ("lq", 5), ("l", 6), ("t", 7), ("lq", 6), ("l", 7), ("lq", 7), ("ev", 1, 1), ("ev", 3, 1), ("ev", 5, 1), ("ev", 7, 1)],
+            "S": [("I", 1), ("Y", 0), ("d", 0, 0, 0), ("r", 0), ("d", 0, 0, 1), ("d", 0, 1, 0), ("d", 0, 1, 1), ("I", 2), ("Y", 1), ("d", 1, 0, 0), ("r", 1), ("d", 1, 0, 1), ("d", 1, 1, 0), ("d", 1, 1, 1), ("Y", 2), ("I", 4), ("r", 2), ("I", 5), ("Y", 3), ("I", 7), ("r", 3), ("I", 8), ("Y", 4), ("I", 9), ("r", 4), ("I", 10), ("I", 11), ("Y", 5), ("r", 5), ("ev", 0, 0), ("ev", 1, 0), ("ev", 2, 0), ("ev", 3, 0), ("Y", 6), ("ev", 4, 0), ("ev", 5, 0), ("r", 6), ("ev", 6, 0), ("ev", 7, 0), ("Y", 7), ("r", 7), ("ev", 0, 1), ("ev", 2, 1), ("ev", 4, 1), ("ev", 6, 1)],
+        }
+        pe = [("tr", h, g, p) for h in range(2) for g in range(2) for p in range(2)]
+        for h in range(2):
+            for kind, g in (("f", 0), ("f", 1), ("a", 0), ("a", 1), ("a", 2), ("a", 3)):
+                pe += [("mm", t, h, kind, g) for t in range(NT)]
+        queues["P"] = pe
+
+        def needs(op):
+            n, x = op[0], op[1:]
+            if n == "Q":
+                return [("I",) + x]
+            if n == "d":
+                return [("tr",) + x]
+            if n == "eq":
+                return [("d",) + x + (0,), ("d",) + x + (1,)]
+            if n in ("Y", "r", "t", "l", "lq"):
+                return [({"Y": "w", "r": "Y", "t": "r", "l": "t", "lq": "l"}[n],) + x]
+            if n == "mm":
+                t, h, kind, g = x
+                if kind == "f":
+                    d = [("Q", 2 * g + t // 4), ("eq", h, g)]
+                    if g == 0:
+                        d += [("d", 1, 1, 1)] if h == 0 else [("ev", t, 0)]
+                    return d
+                return [("Q", 4 + 2 * g + t // 4), ("lq", g + 4 * h)]
+            if n == "ev":
+                return [("mm", x[0], x[1], "a", 3)]
+            return []
+
+        done = set()
+        place = {"V": 0, "S": 0, "P": 0}
+        left = sum(len(q) for q in queues.values())
+        while left:
+            for eng in ("P", "V", "S"):
+                q = queues[eng]
+                while place[eng] < len(q) and all(d in done for d in needs(q[place[eng]])):
+                    op = q[place[eng]]
+                    steps[op[0]](eng, *op[1:])
+                    done.add(op)
+                    place[eng] += 1
+                    left -= 1
+                    if op == ("w", 0):
+                        load_ax(6)
+                    if op == ("w", 1):
+                        load_ax(7)

@@ -32,18 +32,14 @@ def tile_log_barrier_gradient_s2_kernel(tc, e, f, ax, b, mu, a, c, out):
         psum = ctx.enter_context(tc.psum_pool(name="psum", bufs=1))
         ctx.enter_context(tc.manual_schedule())
 
-        rows = const.tile([P, P], BF16, name="rows")
+        rows = const.tile([P, H], BF16, name="rows")
         nc.vector.memset(rows[:], 0.0)
-        bcol = const.tile([P, 4, PACK], BF16, name="bcol")
         warm = const.tile([P, 1], F32, name="warm")
-        nc.scalar.dma_start(out=rows[0:8, :], in_=mu.rearrange("(t m) -> t m", m=P))
-        nc.scalar.dma_start(out=rows[8:16, :], in_=c.rearrange("(t m) -> t m", m=P))
-        nc.scalar.dma_start(out=bcol[:], in_=b.rearrange("(g p j) -> p g j", p=P, j=PACK))
+        nc.vector.memset(warm[:], 1.0)
         ident_b = const.tile([P, P], BF16, name="ident_b")
         make_identity(nc, ident_b[:])
         ident_f = const.tile([P, P], F32, name="ident_f")
         make_identity(nc, ident_f[:])
-        nc.vector.memset(warm[:], 1.0)
         nc.scalar.activation(out=warm[:], in_=warm[:], func=ACT.Abs_reciprocal_sqrt)
 
         fraw = {}
@@ -79,6 +75,9 @@ def tile_log_barrier_gradient_s2_kernel(tc, e, f, ax, b, mu, a, c, out):
             axraw[k] = t
 
         load_f(0, 0)
+        nc.sync.dma_start(out=rows[0:4, :], in_=b.rearrange("(g m) -> g m", m=H))
+        nc.sync.dma_start(out=rows[4:12, 0:P], in_=mu.rearrange("(t m) -> t m", m=P))
+        nc.sync.dma_start(out=rows[12:20, 0:P], in_=c.rearrange("(t m) -> t m", m=P))
         load_ax(0)
         load_f(0, 1)
         load_e(0)
@@ -105,15 +104,19 @@ def tile_log_barrier_gradient_s2_kernel(tc, e, f, ax, b, mu, a, c, out):
         ls = [keep.tile([P, R], U8, name=f"ls{g}", align_bytes=64) for g in range(4)]
         qrow = const.tile([P, R], F32, name="qrow")
         qcol = const.tile([P, 8], F32, name="qcol")
+        bcol = const.tile([P, 4, PACK], F32, name="bcol")
         ccol = const.tile([P, 8], F32, name="ccol")
 
         def bank(i, shape, dtype, nm):
             return psum.tile(shape, dtype, name=nm, tag=f"bank{i}")
 
-        vt = bank(0, [P, P], BF16, "vt")
-        nc.tensor.transpose(vt[:], rows[:], ident_b[:])
-        nc.vector.reciprocal(out=qcol[:], in_=vt[:, 0:8])
-        nc.vector.tensor_copy(out=ccol[:], in_=vt[:, 8:16])
+        vt = bank(0, [P, PACK + 1, P], BF16, "vt")
+        nc.tensor.transpose(vt[:, PACK, :], rows[:, 0:P], ident_b[:])
+        for j in range(PACK):
+            nc.tensor.transpose(vt[:, j, :], rows[:, j:H:PACK], ident_b[:])
+        nc.vector.reciprocal(out=qcol[:], in_=vt[:, PACK, 4:12])
+        nc.vector.tensor_copy(out=bcol[:].rearrange("p g j -> p j g"), in_=vt[:, 0:PACK, 0:4])
+        nc.vector.tensor_copy(out=ccol[:], in_=vt[:, PACK, 12:20])
         for hh in range(2):
             qp = bank(1 + hh, [P, H], F32, f"qp{hh}")
             for t in range(4):
@@ -219,7 +222,10 @@ def tile_log_barrier_gradient_s2_kernel(tc, e, f, ax, b, mu, a, c, out):
             t = stage.tile([P, H, PACK], F32, name=f"t{k}", tag="t", bufs=1)
             tt[k] = t
             nc.vector.tensor_tensor(
-                out=t[:], in0=wt.pop(k)[:].rearrange("p t w -> p w t"), in1=rt[k][:], op=ALU.mult
+                out=t[:].rearrange("p (w i) t -> p w t i", i=4),
+                in0=wt.pop(k)[:].rearrange("p t (w i) -> p w t i", i=4),
+                in1=rt[k][:].rearrange("p (w i) t -> p w t i", i=4),
+                op=ALU.mult,
             )
 
         def step_l(eng, k):
@@ -269,8 +275,8 @@ def tile_log_barrier_gradient_s2_kernel(tc, e, f, ax, b, mu, a, c, out):
         }
 
         queues = {
-            "V": [("I", 0), ("Q", 0), ("w", 0), ("Q", 1), ("w", 1), ("I", 3), ("t", 0), ("Q", 3), ("l", 0), ("eq", 0, 0), ("eq", 0, 1), ("lq", 0), ("Q", 2), ("w", 2), ("w", 3), ("t", 1), ("eq", 1, 0), ("eq", 1, 1), ("l", 1), ("I", 6), ("lq", 1), ("Q", 4), ("t", 2), ("Q", 5), ("l", 2), ("w", 4), ("lq", 2), ("Q", 6), ("Q", 7), ("t", 3), ("w", 5), ("l", 3), ("Q", 8), ("lq", 3), ("Q", 9), ("t", 4), ("Q", 10), ("w", 6), ("l", 4), ("Q", 11), ("lq", 4), ("t", 5), ("w", 7), ("l", 5), ("t", 6), ("lq", 5), ("l", 6), ("t", 7), ("lq", 6), ("l", 7), ("lq", 7), ("ev", 1, 1), ("ev", 3, 1), ("ev", 5, 1), ("ev", 7, 1)],
-            "S": [("I", 1), ("Y", 0), ("d", 0, 0, 0), ("r", 0), ("d", 0, 0, 1), ("d", 0, 1, 0), ("d", 0, 1, 1), ("I", 2), ("Y", 1), ("d", 1, 0, 0), ("r", 1), ("d", 1, 0, 1), ("d", 1, 1, 0), ("d", 1, 1, 1), ("Y", 2), ("I", 4), ("r", 2), ("I", 5), ("Y", 3), ("I", 7), ("r", 3), ("I", 8), ("Y", 4), ("I", 9), ("r", 4), ("I", 10), ("I", 11), ("Y", 5), ("r", 5), ("ev", 0, 0), ("ev", 1, 0), ("ev", 2, 0), ("ev", 3, 0), ("Y", 6), ("ev", 4, 0), ("ev", 5, 0), ("r", 6), ("ev", 6, 0), ("ev", 7, 0), ("Y", 7), ("r", 7), ("ev", 0, 1), ("ev", 2, 1), ("ev", 4, 1), ("ev", 6, 1)],
+            "V": [("I", 0), ("w", 0), ("Q", 0), ("Q", 1), ("w", 1), ("I", 3), ("t", 0), ("Q", 3), ("l", 0), ("eq", 0, 0), ("eq", 0, 1), ("lq", 0), ("Q", 2), ("w", 2), ("w", 3), ("t", 1), ("eq", 1, 0), ("eq", 1, 1), ("l", 1), ("I", 6), ("lq", 1), ("Q", 4), ("t", 2), ("Q", 5), ("l", 2), ("w", 4), ("lq", 2), ("Q", 6), ("Q", 7), ("t", 3), ("w", 5), ("l", 3), ("Q", 8), ("lq", 3), ("Q", 9), ("t", 4), ("Q", 10), ("w", 6), ("l", 4), ("Q", 11), ("lq", 4), ("t", 5), ("w", 7), ("l", 5), ("t", 6), ("lq", 5), ("l", 6), ("t", 7), ("lq", 6), ("l", 7), ("lq", 7), ("ev", 1, 1), ("ev", 3, 1), ("ev", 5, 1), ("ev", 7, 1)],
+            "S": [("I", 1), ("Y", 0), ("d", 0, 0, 0), ("d", 0, 0, 1), ("r", 0), ("d", 0, 1, 0), ("d", 0, 1, 1), ("I", 2), ("Y", 1), ("d", 1, 0, 0), ("r", 1), ("d", 1, 0, 1), ("d", 1, 1, 0), ("d", 1, 1, 1), ("Y", 2), ("I", 4), ("r", 2), ("I", 5), ("Y", 3), ("I", 7), ("r", 3), ("I", 8), ("Y", 4), ("I", 9), ("r", 4), ("I", 10), ("I", 11), ("Y", 5), ("ev", 0, 0), ("ev", 1, 0), ("r", 5), ("ev", 2, 0), ("ev", 3, 0), ("Y", 6), ("ev", 4, 0), ("r", 6), ("ev", 5, 0), ("ev", 6, 0), ("ev", 7, 0), ("Y", 7), ("r", 7), ("ev", 0, 1), ("ev", 2, 1), ("ev", 4, 1), ("ev", 6, 1)],
         }
         pe = [("tr", h, g, p) for h in range(2) for g in range(2) for p in range(2)]
         for h in range(2):

@@ -180,11 +180,11 @@ def tile_log_barrier_gradient_s2_kernel(tc, e, f, ax, b, mu, a, c, out):
             if pr == 0:
                 egr[(h, g)] = stage.tile([P, H, PACK], BF16, name=f"eg{h}{g}", tag="eg", bufs=2, align_bytes=64)
             nc.scalar.copy(
-                out=egr[(h, g)][:, 256 * pr : 256 * (pr + 1), :]
+                out=egr[(h, g)][:]
                 .rearrange("p r t -> p (r t)")
                 .bitcast(F32)
-                .rearrange("p (r u) -> p r u", u=2),
-                in_=xts.pop((h, g, pr))[:].rearrange("p u r -> p r u"),
+                .rearrange("p (i w u) -> p i w u", i=4, u=2)[:, :, 64 * pr : 64 * (pr + 1), :],
+                in_=xts.pop((h, g, pr))[:].rearrange("p u (w i) -> p i w u", i=4),
             )
 
         def step_eq(eng, h, g):
@@ -210,29 +210,31 @@ def tile_log_barrier_gradient_s2_kernel(tc, e, f, ax, b, mu, a, c, out):
             nc.scalar.activation(out=y[:], in_=wt[k][:], func=ACT.Abs_reciprocal_sqrt, scale=-1.0)
 
         def step_r(eng, k):
-            r = stage.tile([P, H, PACK], F32, name=f"r{k}", tag="r", bufs=2)
+            r = stage.tile([P, P, PACK, 4], F32, name=f"r{k}", tag="r", bufs=2)
             rt[k] = r
             nc.scalar.activation(
-                out=r[:].rearrange("p (w i) t -> p w t i", i=4),
+                out=r[:],
                 in_=yt.pop(k)[:].rearrange("p t (w i) -> p w t i", i=4),
                 func=ACT.Square,
             )
 
         def step_t(eng, k):
-            t = stage.tile([P, H, PACK], F32, name=f"t{k}", tag="t", bufs=1)
+            t = stage.tile([P, P, PACK, 4], F32, name=f"t{k}", tag="t", bufs=1)
             tt[k] = t
             nc.vector.tensor_tensor(
-                out=t[:].rearrange("p (w i) t -> p w t i", i=4),
-                in0=wt.pop(k)[:].rearrange("p t (w i) -> p w t i", i=4),
-                in1=rt[k][:].rearrange("p (w i) t -> p w t i", i=4),
-                op=ALU.mult,
+                out=t[:], in0=wt.pop(k)[:].rearrange("p t (w i) -> p w t i", i=4), in1=rt[k][:], op=ALU.mult
             )
 
         def step_l(eng, k):
             lt = stage.tile([P, H, PACK], BF16, name=f"lam{k}", tag="lam", bufs=2, align_bytes=64)
             lam[k] = lt
             nc.vector.scalar_tensor_tensor(
-                out=lt[:], in0=tt.pop(k)[:], scalar=2.0, in1=rt.pop(k)[:], op0=ALU.add, op1=ALU.mult
+                out=lt[:].rearrange("p (i w) t -> p i (w t)", i=4),
+                in0=tt.pop(k)[:].rearrange("p w t i -> p i (w t)"),
+                scalar=2.0,
+                in1=rt.pop(k)[:].rearrange("p w t i -> p i (w t)"),
+                op0=ALU.add,
+                op1=ALU.mult,
             )
 
         def step_lq(eng, k):
@@ -261,11 +263,18 @@ def tile_log_barrier_gradient_s2_kernel(tc, e, f, ax, b, mu, a, c, out):
             o = stage.tile([P, H], F32, name=f"o{t}{h}", tag="o", bufs=4)
             if eng == "V":
                 nc.vector.tensor_scalar(
-                    out=o[:], in0=acc[(t, h)][:], scalar1=ccol[:, t : t + 1], scalar2=None, op0=ALU.add
+                    out=o[:].rearrange("p (w i) -> p w i", i=4),
+                    in0=acc[(t, h)][:].rearrange("p (i w) -> p w i", i=4),
+                    scalar1=ccol[:, t : t + 1],
+                    scalar2=None,
+                    op0=ALU.add,
                 )
             else:
                 nc.scalar.activation(
-                    out=o[:], in_=acc[(t, h)][:], func=ACT.Identity, bias=ccol[:, t : t + 1]
+                    out=o[:].rearrange("p (w i) -> p w i", i=4),
+                    in_=acc[(t, h)][:].rearrange("p (i w) -> p w i", i=4),
+                    func=ACT.Identity,
+                    bias=ccol[:, t : t + 1],
                 )
             nc.sync.dma_start(out=out[P * t : P * (t + 1), H * h : H * (h + 1)], in_=o[:])
 

@@ -183,8 +183,8 @@ def tile_log_barrier_gradient_s2_kernel(tc, e, f, ax, b, mu, a, c, out):
                 out=egr[(h, g)][:]
                 .rearrange("p r t -> p (r t)")
                 .bitcast(F32)
-                .rearrange("p (i w u) -> p i w u", i=4, u=2)[:, :, 64 * pr : 64 * (pr + 1), :],
-                in_=xts.pop((h, g, pr))[:].rearrange("p u (w i) -> p i w u", i=4),
+                .rearrange("p (i w u) -> p i w u", i=2, u=2)[:, :, P * pr : P * (pr + 1), :],
+                in_=xts.pop((h, g, pr))[:].rearrange("p u (w i) -> p i w u", i=2),
             )
 
         def step_eq(eng, h, g):
@@ -210,26 +210,26 @@ def tile_log_barrier_gradient_s2_kernel(tc, e, f, ax, b, mu, a, c, out):
             nc.scalar.activation(out=y[:], in_=wt[k][:], func=ACT.Abs_reciprocal_sqrt, scale=-1.0)
 
         def step_r(eng, k):
-            r = stage.tile([P, P, PACK, 4], F32, name=f"r{k}", tag="r", bufs=2)
+            r = stage.tile([P, 256, PACK, 2], F32, name=f"r{k}", tag="r", bufs=2)
             rt[k] = r
             nc.scalar.activation(
                 out=r[:],
-                in_=yt.pop(k)[:].rearrange("p t (w i) -> p w t i", i=4),
+                in_=yt.pop(k)[:].rearrange("p t (w i) -> p w t i", i=2),
                 func=ACT.Square,
             )
 
         def step_t(eng, k):
-            t = stage.tile([P, P, PACK, 4], F32, name=f"t{k}", tag="t", bufs=1)
+            t = stage.tile([P, 256, PACK, 2], F32, name=f"t{k}", tag="t", bufs=1)
             tt[k] = t
             nc.vector.tensor_tensor(
-                out=t[:], in0=wt.pop(k)[:].rearrange("p t (w i) -> p w t i", i=4), in1=rt[k][:], op=ALU.mult
+                out=t[:], in0=wt.pop(k)[:].rearrange("p t (w i) -> p w t i", i=2), in1=rt[k][:], op=ALU.mult
             )
 
         def step_l(eng, k):
             lt = stage.tile([P, H, PACK], BF16, name=f"lam{k}", tag="lam", bufs=2, align_bytes=64)
             lam[k] = lt
             nc.vector.scalar_tensor_tensor(
-                out=lt[:].rearrange("p (i w) t -> p i (w t)", i=4),
+                out=lt[:].rearrange("p (i w) t -> p i (w t)", i=2),
                 in0=tt.pop(k)[:].rearrange("p w t i -> p i (w t)"),
                 scalar=2.0,
                 in1=rt.pop(k)[:].rearrange("p w t i -> p i (w t)"),
@@ -263,16 +263,16 @@ def tile_log_barrier_gradient_s2_kernel(tc, e, f, ax, b, mu, a, c, out):
             o = stage.tile([P, H], F32, name=f"o{t}{h}", tag="o", bufs=4)
             if eng == "V":
                 nc.vector.tensor_scalar(
-                    out=o[:].rearrange("p (w i) -> p w i", i=4),
-                    in0=acc[(t, h)][:].rearrange("p (i w) -> p w i", i=4),
+                    out=o[:].rearrange("p (w i) -> p w i", i=2),
+                    in0=acc[(t, h)][:].rearrange("p (i w) -> p w i", i=2),
                     scalar1=ccol[:, t : t + 1],
                     scalar2=None,
                     op0=ALU.add,
                 )
             else:
                 nc.scalar.activation(
-                    out=o[:].rearrange("p (w i) -> p w i", i=4),
-                    in_=acc[(t, h)][:].rearrange("p (i w) -> p w i", i=4),
+                    out=o[:].rearrange("p (w i) -> p w i", i=2),
+                    in_=acc[(t, h)][:].rearrange("p (i w) -> p w i", i=2),
                     func=ACT.Identity,
                     bias=ccol[:, t : t + 1],
                 )
@@ -284,8 +284,8 @@ def tile_log_barrier_gradient_s2_kernel(tc, e, f, ax, b, mu, a, c, out):
         }
 
         queues = {
-            "V": [("I", 0), ("w", 0), ("Q", 0), ("Q", 1), ("w", 1), ("I", 3), ("t", 0), ("Q", 3), ("l", 0), ("eq", 0, 0), ("eq", 0, 1), ("lq", 0), ("Q", 2), ("w", 2), ("w", 3), ("t", 1), ("eq", 1, 0), ("eq", 1, 1), ("l", 1), ("I", 6), ("lq", 1), ("Q", 4), ("t", 2), ("Q", 5), ("l", 2), ("w", 4), ("lq", 2), ("Q", 6), ("Q", 7), ("t", 3), ("w", 5), ("l", 3), ("Q", 8), ("lq", 3), ("Q", 9), ("t", 4), ("Q", 10), ("w", 6), ("l", 4), ("Q", 11), ("lq", 4), ("t", 5), ("w", 7), ("l", 5), ("t", 6), ("lq", 5), ("l", 6), ("t", 7), ("lq", 6), ("l", 7), ("lq", 7), ("ev", 1, 1), ("ev", 3, 1), ("ev", 5, 1), ("ev", 7, 1)],
-            "S": [("I", 1), ("Y", 0), ("d", 0, 0, 0), ("d", 0, 0, 1), ("r", 0), ("d", 0, 1, 0), ("d", 0, 1, 1), ("I", 2), ("Y", 1), ("d", 1, 0, 0), ("r", 1), ("d", 1, 0, 1), ("d", 1, 1, 0), ("d", 1, 1, 1), ("Y", 2), ("I", 4), ("r", 2), ("I", 5), ("Y", 3), ("I", 7), ("r", 3), ("I", 8), ("Y", 4), ("I", 9), ("r", 4), ("I", 10), ("I", 11), ("Y", 5), ("ev", 0, 0), ("ev", 1, 0), ("r", 5), ("ev", 2, 0), ("ev", 3, 0), ("Y", 6), ("ev", 4, 0), ("r", 6), ("ev", 5, 0), ("ev", 6, 0), ("ev", 7, 0), ("Y", 7), ("r", 7), ("ev", 0, 1), ("ev", 2, 1), ("ev", 4, 1), ("ev", 6, 1)],
+            "V": [("I", 0), ("w", 0), ("Q", 0), ("Q", 1), ("w", 1), ("I", 3), ("t", 0), ("Q", 3), ("l", 0), ("eq", 0, 0), ("eq", 0, 1), ("lq", 0), ("Q", 2), ("w", 2), ("w", 3), ("t", 1), ("eq", 1, 0), ("l", 1), ("I", 6), ("lq", 1), ("eq", 1, 1), ("Q", 4), ("t", 2), ("Q", 5), ("l", 2), ("w", 4), ("lq", 2), ("Q", 6), ("Q", 7), ("t", 3), ("w", 5), ("l", 3), ("Q", 8), ("lq", 3), ("Q", 9), ("t", 4), ("Q", 10), ("w", 6), ("l", 4), ("Q", 11), ("lq", 4), ("t", 5), ("w", 7), ("l", 5), ("t", 6), ("lq", 5), ("l", 6), ("t", 7), ("lq", 6), ("l", 7), ("lq", 7), ("ev", 1, 1), ("ev", 3, 1), ("ev", 5, 1), ("ev", 7, 1)],
+            "S": [("I", 1), ("Y", 0), ("r", 0), ("d", 0, 0, 0), ("d", 0, 0, 1), ("d", 0, 1, 0), ("d", 0, 1, 1), ("I", 2), ("Y", 1), ("d", 1, 0, 0), ("r", 1), ("d", 1, 0, 1), ("d", 1, 1, 0), ("d", 1, 1, 1), ("Y", 2), ("I", 4), ("r", 2), ("I", 5), ("Y", 3), ("I", 7), ("r", 3), ("I", 8), ("Y", 4), ("I", 9), ("r", 4), ("I", 10), ("I", 11), ("Y", 5), ("ev", 0, 0), ("ev", 1, 0), ("r", 5), ("ev", 2, 0), ("ev", 3, 0), ("Y", 6), ("ev", 4, 0), ("ev", 5, 0), ("r", 6), ("ev", 6, 0), ("ev", 7, 0), ("Y", 7), ("r", 7), ("ev", 0, 1), ("ev", 2, 1), ("ev", 4, 1), ("ev", 6, 1)],
         }
         pe = [("tr", h, g, p) for h in range(2) for g in range(2) for p in range(2)]
         for h in range(2):

@@ -48,7 +48,7 @@ def tile_log_barrier_gradient_s2_kernel(tc, e, f, ax, b, mu, a, c, out):
         axraw = {}
 
         def load_f(g, hh):
-            t = raw.tile([P, PACK, H], BF16, name=f"f{g}{hh}")
+            t = raw.tile([P, PACK, H], BF16, name=f"f{g}{hh}", tag="raw4", bufs=8)
             nc.sync.dma_start(
                 out=t[:],
                 in_=f[512 * g : 512 * (g + 1), H * hh : H * (hh + 1)].rearrange("(p j) n -> p j n", j=PACK),
@@ -56,18 +56,18 @@ def tile_log_barrier_gradient_s2_kernel(tc, e, f, ax, b, mu, a, c, out):
             fraw[(g, hh)] = t
 
         def load_a(g):
-            t = raw.tile([P, PACK, N], BF16, name=f"a{g}", tag="raw8", bufs=4)
+            t = raw.tile([P, PACK, N], BF16, name=f"a{g}", tag="raw8", bufs=3)
             nc.sync.dma_start(out=t[:], in_=a[512 * g : 512 * (g + 1), :].rearrange("(p j) n -> p j n", j=PACK))
             araw[g] = t
 
         def load_e(h):
-            t = raw.tile([P, 4, L], BF16, name=f"e{h}", tag="raw8", bufs=4)
+            t = raw.tile([P, 4, L], BF16, name=f"e{h}", tag="raw8", bufs=3)
             nc.sync.dma_start(out=t[:], in_=e[512 * h : 512 * (h + 1), :].rearrange("(t p) l -> p t l", p=P))
             eraw[h] = t
 
         def load_ax(k):
             g, h = k % 4, k // 4
-            t = raw.tile([P, PACK, H], BF16, name=f"ax{k}", tag="ax", bufs=6)
+            t = raw.tile([P, PACK, H], BF16, name=f"ax{k}", tag="raw4", bufs=8)
             nc.sync.dma_start(
                 out=t[:],
                 in_=ax[512 * g : 512 * (g + 1), H * h : H * (h + 1)].rearrange("(p j) r -> p j r", j=PACK),
@@ -80,19 +80,21 @@ def tile_log_barrier_gradient_s2_kernel(tc, e, f, ax, b, mu, a, c, out):
         nc.sync.dma_start(out=rows[12:20, 0:P], in_=c.rearrange("(t m) -> t m", m=P))
         load_ax(0)
         load_f(0, 1)
-        load_e(0)
         load_ax(1)
         load_f(1, 0)
+        load_ax(2)
         load_f(1, 1)
+        load_ax(3)
+        load_e(0)
         load_e(1)
         load_a(0)
-        load_ax(2)
         load_a(1)
-        load_ax(3)
         load_a(2)
         load_ax(4)
         load_a(3)
         load_ax(5)
+        load_ax(6)
+        load_ax(7)
 
         fc = [keep.tile([P, N], U32, name=f"fc{g}", align_bytes=64) for g in range(2)]
         fs = [keep.tile([P, N], U8, name=f"fs{g}", align_bytes=64) for g in range(2)]
@@ -102,7 +104,7 @@ def tile_log_barrier_gradient_s2_kernel(tc, e, f, ax, b, mu, a, c, out):
         es = [keep.tile([P, R], U8, name=f"es{g}", align_bytes=64) for g in range(2)]
         lc = [keep.tile([P, R], U32, name=f"lc{g}", align_bytes=64) for g in range(4)]
         ls = [keep.tile([P, R], U8, name=f"ls{g}", align_bytes=64) for g in range(4)]
-        qrow = const.tile([P, R], F32, name="qrow")
+        qrow = const.tile([P, H], F32, name="qrow")
         qcol = const.tile([P, 8], F32, name="qcol")
         bcol = const.tile([P, 4, PACK], F32, name="bcol")
         ccol = const.tile([P, 8], F32, name="ccol")
@@ -117,15 +119,16 @@ def tile_log_barrier_gradient_s2_kernel(tc, e, f, ax, b, mu, a, c, out):
         nc.vector.reciprocal(out=qcol[:], in_=vt[:, PACK, 4:12])
         nc.vector.tensor_copy(out=bcol[:].rearrange("p g j -> p j g"), in_=vt[:, 0:PACK, 0:4])
         nc.vector.tensor_copy(out=ccol[:], in_=vt[:, PACK, 12:20])
+        qps = [bank(7, [P, H], F32, "qp0"), bank(1, [P, H], F32, "qp1")]
         for hh in range(2):
-            qp = bank(1 + hh, [P, H], F32, f"qp{hh}")
+            qp = qps[hh]
             for t in range(4):
                 nc.tensor.transpose(
                     qp[:, P * t : P * (t + 1)],
                     qcol[:, 4 * hh + t : 4 * hh + t + 1].to_broadcast([P, P]),
                     ident_f[:],
                 )
-            nc.scalar.copy(out=qrow[:, H * hh : H * (hh + 1)], in_=qp[:])
+        nc.scalar.copy(out=qrow[:], in_=qps[1][:])
 
         grouped = {}
         egr = {}
@@ -145,11 +148,21 @@ def tile_log_barrier_gradient_s2_kernel(tc, e, f, ax, b, mu, a, c, out):
 
         def step_I(eng, u):
             src = unit(u)[0]
-            g = stage.tile([P, H, PACK], BF16, name=f"grp{u}", tag="grp" + eng, bufs=2 if eng == "V" else 3, align_bytes=64)
+            g = stage.tile([P, H, PACK], BF16, name=f"grp{u}", tag="grp", bufs=5, align_bytes=64)
             grouped[u] = g
             o = g[:].rearrange("p (w i) t -> p w t i", i=4)
             i = src.rearrange("p t (w i) -> p w t i", i=4)
-            if eng == "V":
+            if eng == "G":
+                for x in (slice(0, 256), slice(256, 512)):
+                    nc.gpsimd.tensor_scalar(
+                        out=g[:, x, :],
+                        in0=src[:, :, x].rearrange("p t w -> p w t"),
+                        scalar1=1.0,
+                        scalar2=0.0,
+                        op0=ALU.mult,
+                        op1=ALU.add,
+                    )
+            elif eng == "V":
                 nc.vector.tensor_copy(out=o, in_=i)
             else:
                 nc.scalar.copy(out=o, in_=i)
@@ -192,14 +205,14 @@ def tile_log_barrier_gradient_s2_kernel(tc, e, f, ax, b, mu, a, c, out):
 
         def step_w(eng, k):
             g, h = k % 4, k // 4
-            w = stage.tile([P, PACK, H], F32, name=f"w{k}", tag="w", bufs=3)
+            w = stage.tile([P, PACK, H], F32, name=f"w{k}", tag="w", bufs=4)
             wt[k] = w
             for j in range(PACK):
                 nc.vector.scalar_tensor_tensor(
                     out=w[:, j, :],
                     in0=axraw[k][:, j, :],
                     scalar=bcol[:, g, j : j + 1],
-                    in1=qrow[:, H * h : H * (h + 1)],
+                    in1=(qps[0] if h == 0 else qrow)[:],
                     op0=ALU.subtract,
                     op1=ALU.mult,
                 )
@@ -260,7 +273,7 @@ def tile_log_barrier_gradient_s2_kernel(tc, e, f, ax, b, mu, a, c, out):
             )
 
         def step_ev(eng, t, h):
-            o = stage.tile([P, H], F32, name=f"o{t}{h}", tag="o", bufs=4)
+            o = raw.tile([P, H], F32, name=f"o{t}{h}", tag="raw4", bufs=8)
             if eng == "V":
                 nc.vector.tensor_scalar(
                     out=o[:].rearrange("p (w i) -> p w i", i=2),
@@ -284,8 +297,9 @@ def tile_log_barrier_gradient_s2_kernel(tc, e, f, ax, b, mu, a, c, out):
         }
 
         queues = {
-            "V": [("I", 0), ("w", 0), ("Q", 0), ("Q", 1), ("w", 1), ("I", 3), ("t", 0), ("Q", 3), ("l", 0), ("eq", 0, 0), ("eq", 0, 1), ("lq", 0), ("Q", 2), ("w", 2), ("w", 3), ("t", 1), ("eq", 1, 0), ("l", 1), ("I", 6), ("lq", 1), ("eq", 1, 1), ("Q", 4), ("t", 2), ("Q", 5), ("l", 2), ("w", 4), ("lq", 2), ("Q", 6), ("Q", 7), ("t", 3), ("w", 5), ("l", 3), ("Q", 8), ("lq", 3), ("Q", 9), ("t", 4), ("Q", 10), ("w", 6), ("l", 4), ("Q", 11), ("lq", 4), ("t", 5), ("w", 7), ("l", 5), ("t", 6), ("lq", 5), ("l", 6), ("t", 7), ("lq", 6), ("l", 7), ("lq", 7), ("ev", 1, 1), ("ev", 3, 1), ("ev", 5, 1), ("ev", 7, 1)],
-            "S": [("I", 1), ("Y", 0), ("r", 0), ("d", 0, 0, 0), ("d", 0, 0, 1), ("d", 0, 1, 0), ("d", 0, 1, 1), ("I", 2), ("Y", 1), ("d", 1, 0, 0), ("r", 1), ("d", 1, 0, 1), ("d", 1, 1, 0), ("d", 1, 1, 1), ("Y", 2), ("I", 4), ("r", 2), ("I", 5), ("Y", 3), ("I", 7), ("r", 3), ("I", 8), ("Y", 4), ("I", 9), ("r", 4), ("I", 10), ("I", 11), ("Y", 5), ("ev", 0, 0), ("ev", 1, 0), ("r", 5), ("ev", 2, 0), ("ev", 3, 0), ("Y", 6), ("ev", 4, 0), ("ev", 5, 0), ("r", 6), ("ev", 6, 0), ("ev", 7, 0), ("Y", 7), ("r", 7), ("ev", 0, 1), ("ev", 2, 1), ("ev", 4, 1), ("ev", 6, 1)],
+            "V": [("w", 0), ("w", 1), ("Q", 0), ("w", 2), ("w", 3), ("t", 0), ("Q", 1), ("l", 0), ("Q", 2), ("t", 1), ("lq", 0), ("Q", 3), ("l", 1), ("I", 8), ("Q", 4), ("lq", 1), ("w", 4), ("t", 2), ("Q", 5), ("eq", 0, 0), ("l", 2), ("eq", 0, 1), ("lq", 2), ("Q", 6), ("w", 5), ("t", 3), ("Q", 7), ("l", 3), ("Q", 8), ("lq", 3), ("w", 6), ("t", 4), ("Q", 9), ("eq", 1, 0), ("l", 4), ("eq", 1, 1), ("lq", 4), ("Q", 10), ("w", 7), ("t", 5), ("Q", 11), ("l", 5), ("t", 6), ("lq", 5), ("l", 6), ("t", 7), ("lq", 6), ("l", 7), ("lq", 7), ("ev", 1, 1), ("ev", 3, 1), ("ev", 5, 1), ("ev", 7, 1)],
+            "S": [("Y", 0), ("r", 0), ("Y", 1), ("r", 1), ("d", 0, 0, 0), ("d", 0, 0, 1), ("d", 0, 1, 0), ("d", 0, 1, 1), ("Y", 2), ("I", 4), ("r", 2), ("I", 5), ("I", 6), ("I", 7), ("Y", 3), ("r", 3), ("d", 1, 0, 0), ("d", 1, 0, 1), ("d", 1, 1, 0), ("d", 1, 1, 1), ("Y", 4), ("I", 9), ("r", 4), ("I", 10), ("I", 11), ("Y", 5), ("r", 5), ("Y", 6), ("ev", 0, 0), ("ev", 1, 0), ("ev", 2, 0), ("r", 6), ("ev", 3, 0), ("ev", 4, 0), ("ev", 5, 0), ("ev", 6, 0), ("ev", 7, 0), ("Y", 7), ("r", 7), ("ev", 0, 1), ("ev", 2, 1), ("ev", 4, 1), ("ev", 6, 1)],
+            "G": [("I", 0), ("I", 1), ("I", 2), ("I", 3)],
         }
         pe = [("tr", h, g, p) for h in range(2) for g in range(2) for p in range(2)]
         for h in range(2):
@@ -316,10 +330,10 @@ def tile_log_barrier_gradient_s2_kernel(tc, e, f, ax, b, mu, a, c, out):
             return []
 
         done = set()
-        place = {"V": 0, "S": 0, "P": 0}
+        place = {"V": 0, "S": 0, "P": 0, "G": 0}
         left = sum(len(q) for q in queues.values())
         while left:
-            for eng in ("P", "V", "S"):
+            for eng in ("G", "P", "V", "S"):
                 q = queues[eng]
                 while place[eng] < len(q) and all(d in done for d in needs(q[place[eng]])):
                     op = q[place[eng]]
@@ -327,7 +341,3 @@ def tile_log_barrier_gradient_s2_kernel(tc, e, f, ax, b, mu, a, c, out):
                     done.add(op)
                     place[eng] += 1
                     left -= 1
-                    if op == ("w", 0):
-                        load_ax(6)
-                    if op == ("w", 1):
-                        load_ax(7)

from contextlib import ExitStack

import concourse.mybir as mybir
from concourse.masks import make_identity

N, R, L, M = 1024, 1024, 1024, 2048
FLOPS = 2 * N * R * (L + M)
BYTES = 2 * (R * L + L * N + M * R + M + R + M * N + N) + 4 * N * R

F32 = mybir.dt.float32
BF16 = mybir.dt.bfloat16
U32 = mybir.dt.uint32
U8 = mybir.dt.uint8
E4M3 = mybir.dt.float8_e4m3fn_x4
E5M2 = mybir.dt.float8_e5m2_x4
ALU = mybir.AluOpType
ACT = mybir.ActivationFunctionType

P = 128
PACK = 4
H = 512
NT = N // P


def tile_log_barrier_gradient_s2_kernel(tc, e, f, ax, b, mu, a, c, out):
    nc = tc.nc
    with ExitStack() as ctx:
        const = ctx.enter_context(tc.tile_pool(name="const", bufs=1))
        raw = ctx.enter_context(tc.tile_pool(name="raw", bufs=1))
        keep = ctx.enter_context(tc.tile_pool(name="keep", bufs=1))
        stage = ctx.enter_context(tc.tile_pool(name="stage", bufs=3))
        psum = ctx.enter_context(tc.psum_pool(name="psum", bufs=1))
        ctx.enter_context(tc.manual_schedule())

        rows = const.tile([P, H], BF16, name="rows")
        nc.vector.memset(rows[:], 0.0)
        warm = const.tile([P, 1], F32, name="warm")
        nc.vector.memset(warm[:], 1.0)
        ident_b = const.tile([P, P], BF16, name="ident_b")
        make_identity(nc, ident_b[:])
        ident_f = const.tile([P, P], F32, name="ident_f")
        make_identity(nc, ident_f[:])
        nc.scalar.activation(out=warm[:], in_=warm[:], func=ACT.Abs_reciprocal_sqrt)

        fraw = {}
        araw = {}
        eraw = {}
        axraw = {}

        def load_f(g, hh):
            t = raw.tile([P, PACK, H], BF16, name=f"f{g}{hh}", tag="raw4", bufs=8)
            nc.sync.dma_start(
                out=t[:],
                in_=f[512 * g : 512 * (g + 1), H * hh : H * (hh + 1)].rearrange("(p j) n -> p j n", j=PACK),
            )
            fraw[(g, hh)] = t

        def load_a(g):
            t = raw.tile([P, PACK, N], BF16, name=f"a{g}", tag="raw8", bufs=3)
            nc.sync.dma_start(out=t[:], in_=a[512 * g : 512 * (g + 1), :].rearrange("(p j) n -> p j n", j=PACK))
            araw[g] = t

        def load_e(h):
            t = raw.tile([P, 4, L], BF16, name=f"e{h}", tag="raw8", bufs=3)
            nc.sync.dma_start(out=t[:], in_=e[512 * h : 512 * (h + 1), :].rearrange("(t p) l -> p t l", p=P))
            eraw[h] = t

        def load_ax(k):
            g, h = k % 4, k // 4
            t = raw.tile([P, PACK, H], BF16, name=f"ax{k}", tag="raw4", bufs=8)
            nc.sync.dma_start(
                out=t[:],
                in_=ax[512 * g : 512 * (g + 1), H * h : H * (h + 1)].rearrange("(p j) r -> p j r", j=PACK),
            )
            axraw[k] = t

        load_f(0, 0)
        nc.sync.dma_start(out=rows[0:4, :], in_=b.rearrange("(g m) -> g m", m=H))
        nc.sync.dma_start(out=rows[4:12, 0:P], in_=mu.rearrange("(t m) -> t m", m=P))
        nc.sync.dma_start(out=rows[12:20, 0:P], in_=c.rearrange("(t m) -> t m", m=P))
        load_ax(0)
        load_f(0, 1)
        load_ax(1)
        load_f(1, 0)
        load_ax(2)
        load_f(1, 1)
        load_ax(3)
        load_e(0)
        load_e(1)
        load_a(0)
        load_a(1)
        load_a(2)
        load_ax(4)
        load_a(3)
        load_ax(5)
        load_ax(6)
        load_ax(7)

        fc = [keep.tile([P, N], U32, name=f"fc{g}", align_bytes=64) for g in range(2)]
        fs = [keep.tile([P, N], U8, name=f"fs{g}", align_bytes=64) for g in range(2)]
        ac = [keep.tile([P, N], U32, name=f"ac{g}", align_bytes=64) for g in range(4)]
        asc = [keep.tile([P, N], U8, name=f"as{g}", align_bytes=64) for g in range(4)]
        ec = [keep.tile([P, R], U32, name=f"ec{g}", align_bytes=64) for g in range(2)]
        es = [keep.tile([P, R], U8, name=f"es{g}", align_bytes=64) for g in range(2)]
        lc = [keep.tile([P, R], U32, name=f"lc{g}", align_bytes=64) for g in range(4)]
        ls = [keep.tile([P, R], U8, name=f"ls{g}", align_bytes=64) for g in range(4)]
        qrow = const.tile([P, H], F32, name="qrow")
        qcol = const.tile([P, 8], F32, name="qcol")
        bcol = const.tile([P, 4, PACK], F32, name="bcol")
        ccol = const.tile([P, 8], F32, name="ccol")

        def bank(i, shape, dtype, nm):
            return psum.tile(shape, dtype, name=nm, tag=f"bank{i}")

        vt = bank(0, [P, PACK + 1, P], BF16, "vt")
        nc.tensor.transpose(vt[:, PACK, :], rows[:, 0:P], ident_b[:])
        for j in range(PACK):
            nc.tensor.transpose(vt[:, j, :], rows[:, j:H:PACK], ident_b[:])
        nc.vector.reciprocal(out=qcol[:], in_=vt[:, PACK, 4:12])
        nc.vector.tensor_copy(out=bcol[:].rearrange("p g j -> p j g"), in_=vt[:, 0:PACK, 0:4])
        nc.vector.tensor_copy(out=ccol[:], in_=vt[:, PACK, 12:20])
        qps = [bank(7, [P, H], F32, "qp0"), bank(1, [P, H], F32, "qp1")]
        for hh in range(2):
            qp = qps[hh]
            for t in range(4):
                nc.tensor.transpose(
                    qp[:, P * t : P * (t + 1)],
                    qcol[:, 4 * hh + t : 4 * hh + t + 1].to_broadcast([P, P]),
                    ident_f[:],
                )
        nc.scalar.copy(out=qrow[:], in_=qps[1][:])

        grouped = {}
        egr = {}
        xts = {}
        wt = {}
        yt = {}
        rt = {}
        tt = {}
        lam = {}
        acc = {}

        def unit(u):
            if u < 4:
                return fraw[(u // 2, u % 2)][:], fc[u // 2], fs[u // 2], u % 2
            v = u - 4
            return araw[v // 2][:, :, H * (v % 2) : H * (v % 2 + 1)], ac[v // 2], asc[v // 2], v % 2

        def step_I(eng, u):
            src = unit(u)[0]
            g = stage.tile([P, H, PACK], BF16, name=f"grp{u}", tag="grp", bufs=5, align_bytes=64)
            grouped[u] = g
            o = g[:].rearrange("p (w i) t -> p w t i", i=4)
            i = src.rearrange("p t (w i) -> p w t i", i=4)
            if eng == "G":
                for x in (slice(0, 256), slice(256, 512)):
                    nc.gpsimd.tensor_scalar(
                        out=g[:, x, :],
                        in0=src[:, :, x].rearrange("p t w -> p w t"),
                        scalar1=1.0,
                        scalar2=0.0,
                        op0=ALU.mult,
                        op1=ALU.add,
                    )
            elif eng == "V":
                nc.vector.tensor_copy(out=o, in_=i)
            else:
                nc.scalar.copy(out=o, in_=i)

        def quantize(codes, scales, hh, fmt, src):
            cols = slice(H * hh, H * (hh + 1))
            nc.vector.quantize_mx(
                out=codes[:, cols].bitcast(fmt), scales=scales[:, cols], in_=src[:].rearrange("p w t -> p (w t)")
            )

        def step_Q(eng, u):
            _, codes, scales, hh = unit(u)
            quantize(codes, scales, hh, E4M3, grouped.pop(u))

        def step_tr(eng, h, g, pr):
            words = eraw[h][:].rearrange("p t l -> p (t l)").bitcast(F32).rearrange("p (t w) -> p t w", t=4)
            x = bank(4 * h + 2 * g + pr, [P, 2, 256], F32, f"xt{h}{g}{pr}")
            xts[(h, g, pr)] = x
            for t in range(2):
                for u in range(2):
                    nc.tensor.transpose(
                        x[:, u, P * t : P * (t + 1)],
                        words[:, 2 * pr + t, 256 * g + u : 256 * (g + 1) : 2],
                        ident_f[:],
                    )

        def step_d(eng, h, g, pr):
            if pr == 0:
                egr[(h, g)] = stage.tile([P, H, PACK], BF16, name=f"eg{h}{g}", tag="eg", bufs=2, align_bytes=64)
            nc.scalar.copy(
                out=egr[(h, g)][:]
                .rearrange("p r t -> p (r t)")
                .bitcast(F32)
                .rearrange("p (i w u) -> p i w u", i=2, u=2)[:, :, P * pr : P * (pr + 1), :],
                in_=xts.pop((h, g, pr))[:].rearrange("p u (w i) -> p i w u", i=2),
            )

        def step_eq(eng, h, g):
            quantize(ec[g], es[g], h, E4M3, egr.pop((h, g)))

        def step_w(eng, k):
            g, h = k % 4, k // 4
            w = stage.tile([P, PACK, H], F32, name=f"w{k}", tag="w", bufs=4)
            wt[k] = w
            for j in range(PACK):
                nc.vector.scalar_tensor_tensor(
                    out=w[:, j, :],
                    in0=axraw[k][:, j, :],
                    scalar=bcol[:, g, j : j + 1],
                    in1=(qps[0] if h == 0 else qrow)[:],
                    op0=ALU.subtract,
                    op1=ALU.mult,
                )

        def step_Y(eng, k):
            y = stage.tile([P, PACK, H], F32, name=f"y{k}", tag="y", bufs=1)
            yt[k] = y
            nc.scalar.activation(out=y[:], in_=wt[k][:], func=ACT.Abs_reciprocal_sqrt, scale=-1.0)

        def step_r(eng, k):
            r = stage.tile([P, 256, PACK, 2], F32, name=f"r{k}", tag="r", bufs=2)
            rt[k] = r
            nc.scalar.activation(
                out=r[:],
                in_=yt.pop(k)[:].rearrange("p t (w i) -> p w t i", i=2),
                func=ACT.Square,
            )

        def step_t(eng, k):
            t = stage.tile([P, 256, PACK, 2], F32, name=f"t{k}", tag="t", bufs=1)
            tt[k] = t
            nc.vector.tensor_tensor(
                out=t[:], in0=wt.pop(k)[:].rearrange("p t (w i) -> p w t i", i=2), in1=rt[k][:], op=ALU.mult
            )

        def step_l(eng, k):
            lt = stage.tile([P, H, PACK], BF16, name=f"lam{k}", tag="lam", bufs=2, align_bytes=64)
            lam[k] = lt
            nc.vector.scalar_tensor_tensor(
                out=lt[:].rearrange("p (i w) t -> p i (w t)", i=2),
                in0=tt.pop(k)[:].rearrange("p w t i -> p i (w t)"),
                scalar=2.0,
                in1=rt.pop(k)[:].rearrange("p w t i -> p i (w t)"),
                op0=ALU.add,
                op1=ALU.mult,
            )

        def step_lq(eng, k):
            quantize(lc[k % 4], ls[k % 4], k // 4, E5M2, lam.pop(k))

        def step_mm(eng, t, h, kind, g):
            if kind == "f":
                if g == 0:
                    acc[(t, h)] = bank(t, [P, H], F32, f"acc{t}{h}")
                st, ss, mv, ms, dt = fc[g], fs[g], ec[g], es[g], E4M3
            else:
                st, ss, mv, ms, dt = ac[g], asc[g], lc[g], ls[g], E5M2
            mc = slice(P * t, P * (t + 1))
            rc = slice(H * h, H * (h + 1))
            nc.tensor.matmul_mx(
                out=acc[(t, h)][:],
                lhsT=st[:, mc].bitcast(E4M3),
                lhsT_scale=ss[:, mc],
                rhs=mv[:, rc].bitcast(dt),
                rhs_scale=ms[:, rc],
                start=(kind == "f" and g == 0),
                stop=(kind == "a" and g == 3),
            )

        def step_ev(eng, t, h):
            o = raw.tile([P, H], F32, name=f"o{t}{h}", tag="raw4", bufs=8)
            if eng == "V":
                nc.vector.tensor_scalar(
                    out=o[:].rearrange("p (w i) -> p w i", i=2),
                    in0=acc[(t, h)][:].rearrange("p (i w) -> p w i", i=2),
                    scalar1=ccol[:, t : t + 1],
                    scalar2=None,
                    op0=ALU.add,
                )
            else:
                nc.scalar.activation(
                    out=o[:].rearrange("p (w i) -> p w i", i=2),
                    in_=acc[(t, h)][:].rearrange("p (i w) -> p w i", i=2),
                    func=ACT.Identity,
                    bias=ccol[:, t : t + 1],
                )
            nc.sync.dma_start(out=out[P * t : P * (t + 1), H * h : H * (h + 1)], in_=o[:])

        steps = {
            "I": step_I, "Q": step_Q, "tr": step_tr, "d": step_d, "eq": step_eq, "w": step_w, "Y": step_Y,
            "r": step_r, "t": step_t, "l": step_l, "lq": step_lq, "mm": step_mm, "ev": step_ev,
        }

        queues = {
            "V": [("w", 0), ("w", 1), ("Q", 0), ("w", 2), ("w", 3), ("t", 0), ("Q", 1), ("l", 0), ("Q", 2), ("t", 1), ("lq", 0), ("Q", 3), ("l", 1), ("I", 8), ("Q", 4), ("lq", 1), ("w", 4), ("t", 2), ("Q", 5), ("eq", 0, 0), ("l", 2), ("eq", 0, 1), ("lq", 2), ("Q", 6), ("w", 5), ("t", 3), ("Q", 7), ("l", 3), ("Q", 8), ("lq", 3), ("w", 6), ("t", 4), ("Q", 9), ("eq", 1, 0), ("l", 4), ("eq", 1, 1), ("lq", 4), ("Q", 10), ("w", 7), ("t", 5), ("Q", 11), ("l", 5), ("t", 6), ("lq", 5), ("l", 6), ("t", 7), ("lq", 6), ("l", 7), ("lq", 7), ("ev", 1, 1), ("ev", 3, 1), ("ev", 5, 1), ("ev", 7, 1)],
            "S": [("Y", 0), ("r", 0), ("Y", 1), ("r", 1), ("d", 0, 0, 0), ("d", 0, 0, 1), ("d", 0, 1, 0), ("d", 0, 1, 1), ("Y", 2), ("I", 4), ("r", 2), ("I", 5), ("I", 6), ("I", 7), ("Y", 3), ("r", 3), ("d", 1, 0, 0), ("d", 1, 0, 1), ("d", 1, 1, 0), ("d", 1, 1, 1), ("Y", 4), ("I", 9), ("r", 4), ("I", 10), ("I", 11), ("Y", 5), ("r", 5), ("Y", 6), ("ev", 0, 0), ("ev", 1, 0), ("ev", 2, 0), ("r", 6), ("ev", 3, 0), ("ev", 4, 0), ("ev", 5, 0), ("ev", 6, 0), ("ev", 7, 0), ("Y", 7), ("r", 7), ("ev", 0, 1), ("ev", 2, 1), ("ev", 4, 1), ("ev", 6, 1)],
            "G": [("I", 0), ("I", 1), ("I", 2), ("I", 3)],
        }
        pe = [("tr", h, g, p) for h in range(2) for g in range(2) for p in range(2)]
        for h in range(2):
            for kind, g in (("f", 0), ("f", 1), ("a", 0), ("a", 1), ("a", 2), ("a", 3)):
                pe += [("mm", t, h, kind, g) for t in range(NT)]
        queues["P"] = pe

        def needs(op):
            n, x = op[0], op[1:]
            if n == "Q":
                return [("I",) + x]
            if n == "d":
                return [("tr",) + x]
            if n == "eq":
                return [("d",) + x + (0,), ("d",) + x + (1,)]
            if n in ("Y", "r", "t", "l", "lq"):
                return [({"Y": "w", "r": "Y", "t": "r", "l": "t", "lq": "l"}[n],) + x]
            if n == "mm":
                t, h, kind, g = x
                if kind == "f":
                    d = [("Q", 2 * g + t // 4), ("eq", h, g)]
                    if g == 0:
                        d += [("d", 1, 1, 1)] if h == 0 else [("ev", t, 0)]
                    return d
                return [("Q", 4 + 2 * g + t // 4), ("lq", g + 4 * h)]
            if n == "ev":
                return [("mm", x[0], x[1], "a", 3)]
            return []

        done = set()
        place = {"V": 0, "S": 0, "P": 0, "G": 0}
        left = sum(len(q) for q in queues.values())
        while left:
            for eng in ("G", "P", "V", "S"):
                q = queues[eng]
                while place[eng] < len(q) and all(d in done for d in needs(q[place[eng]])):
                    op = q[place[eng]]
                    steps[op[0]](eng, *op[1:])
                    done.add(op)
                    place[eng] += 1
                    left -= 1
